import numpy as np
import ml_dtypes


def mxq(x, axis, fmt="e4m3"):
    dtype, down = {"e4m3": (ml_dtypes.float8_e4m3fn, 7), "e5m2": (ml_dtypes.float8_e5m2, 14)}[fmt]
    v = np.moveaxis(np.asarray(x, np.float32).astype(ml_dtypes.bfloat16).astype(np.float64), axis, -1)
    blocks = v.reshape(v.shape[:-1] + (-1, 32))
    amax = np.abs(blocks).max(-1, keepdims=True)
    byte = np.maximum(np.where(amax > 0, np.frexp(amax)[1] - 1 + 127, 0) - down, 1)
    scale = np.exp2(byte - 127.0)
    codes = (blocks / scale).astype(np.float32).astype(dtype).astype(np.float64)
    return np.moveaxis((codes * scale).reshape(v.shape), -1, axis)


WIDE = False


def mx_kscale(k):
    if not WIDE:
        return np.ones(k)
    levels = np.array([10, -10, 5, -5, 0])
    if k % 512:
        return np.exp2(np.random.permutation(np.resize(levels, k // 32))).repeat(32)
    a = np.empty((k // 512, 16))
    for p in range(k // 512):
        a[p, :8] = np.random.permutation(np.resize(levels, 8))
        for g in range(8):
            far = levels[np.abs(levels - a[p, g]) >= 10]
            a[p, g + 8] = far[np.random.randint(len(far))]
    return np.exp2(a.ravel()).repeat(32)


def f64(x):
    return np.asarray(x).astype(np.float64)


def striped(idx):
    return np.tile(idx.reshape(-1, 16).T, (8, 1)).astype(np.uint16)


def unstriped(offs):
    return offs[:16].T.reshape(-1).astype(np.int64)


def silu(v):
    return v / (1.0 + np.exp(-np.maximum(v, -700.0)))


K, T, D, S, V, N = 1024, 2048, 16, 512, 32, 512


def setup_inputs():
    n = np.random.standard_normal
    s = mx_kscale(K)[:, None]
    return {
        "xT": (n((K, T)) * s).astype(np.float32),
        "w": (n((K, N)) / np.sqrt(K) / s).astype(np.float32),
        "b": (0.3 * n((N, 1))).astype(np.float32),
        "offs": striped(np.random.permutation(T)[:S]),
    }


def reference(xT, w, b, offs):
    idx = unstriped(offs)
    xq = mxq(f64(xT)[:, idx], 0, "e4m3")
    y = mxq(f64(w), 0, "e4m3").T @ xq
    y = silu(y + f64(b))
    return y.reshape(N, V, D).max(axis=2)

@@ -1,0 +1,188 @@
+from contextlib import ExitStack
+
+import concourse.mybir as mybir
+from concourse.masks import make_identity
+
+K, T, D, S, V, N = 1024, 2048, 16, 512, 32, 512
+FLOPS = 2 * K * N * S
+
+F32 = mybir.dt.float32
+BF16 = mybir.dt.bfloat16
+U32 = mybir.dt.uint32
+U16 = mybir.dt.uint16
+U8 = mybir.dt.uint8
+FP8X4 = mybir.dt.float8_e4m3fn_x4
+SILU = mybir.ActivationFunctionType.Silu
+AX = mybir.AxisListType.X
+MAX = mybir.AluOpType.max
+
+P = 128
+PACK = 4
+K_PASS = P * PACK
+PASSES = K // K_PASS
+M_TILES = N // P
+HALF = S // 2
+
+LOADS = (
+    [("x", 0, 0), ("x", 0, 1)]
+    + [("w", 0, 0, 256)]
+    + [("x", 0, 2), ("x", 0, 3), ("x", 1, 0), ("x", 1, 1), ("x", 1, 2), ("x", 1, 3)]
+    + [("w", 1, 0, 256), ("w", 0, 256, 256), ("w", 1, 256, 128), ("w", 1, 384, 128)]
+)
+
+
+def tile_picked_pool_lin_silu_sub_e_kernel(tc, xT, w, b, offs, out):
+    nc = tc.nc
+    with ExitStack() as ctx:
+        keep = ctx.enter_context(tc.tile_pool(name="keep", bufs=1))
+        psum = ctx.enter_context(tc.psum_pool(name="psum", bufs=1))
+
+        offsets = keep.tile([P, S // 16], U16, name="offsets")
+        nc.sync.dma_start(offsets[:], offs)
+
+        planes = {}
+        raws = {}
+        for item in LOADS:
+            a = item[1]
+            rows = slice(a * K_PASS, (a + 1) * K_PASS)
+            if item[0] == "x":
+                j = item[2]
+                plane = keep.tile([P, T], F32, name=f"plane_{a}_{j}")
+                nc.sync.dma_start(out=plane[:], in_=xT[rows, :].rearrange("(p j) t -> p j t", j=PACK)[:, j, :])
+                planes[(a, j)] = plane
+            else:
+                c, width = item[2], item[3]
+                raw = keep.tile([P, PACK, width], F32, name=f"raw_{a}_{c}")
+                nc.sync.dma_start(out=raw[:], in_=w[rows, c : c + width].rearrange("(p j) n -> p j n", j=PACK))
+                raws[(a, c)] = raw
+
+        warm = keep.tile([P, 1], F32, name="warm")
+        warm_out = keep.tile([P, 1], F32, name="warm_out")
+        nc.vector.memset(warm[:], 0.0)
+        nc.scalar.activation(warm_out[:], warm[:], SILU)
+
+        ident = keep.tile([P, P], F32, name="ident")
+        b_rows = keep.tile([P, P], F32, name="b_rows")
+        bias = keep.tile([P, M_TILES], F32, name="bias")
+        nc.gpsimd.memset(b_rows[:], 0.0)
+        make_identity(nc, ident[:])
+        nc.scalar.dma_start(out=b_rows[0:M_TILES, :], in_=b.rearrange("(t p) o -> t (p o)", t=M_TILES))
+        b_cols = psum.tile([P, P], F32, name="b_cols")
+        nc.tensor.transpose(b_cols[:], b_rows[:], ident[:])
+        nc.vector.tensor_copy(bias[:], b_cols[:, 0:M_TILES])
+
+        x_grouped = []
+        x_codes = []
+        x_scales = []
+        for a in range(PASSES):
+            xg = keep.tile([P, S, PACK], BF16, align_bytes=64, name=f"xg_{a}")
+            xc = keep.tile([P, S], U32, align_bytes=64, name=f"xc_{a}")
+            xs = keep.tile([P, S], U8, align_bytes=64, name=f"xs_{a}")
+            x_grouped.append(xg)
+            x_codes.append(xc)
+            x_scales.append(xs)
+
+        def gather(a, j, n0, n1):
+            nc.vector.tensor_copy(
+                out=x_grouped[a][:, n0:n1, j],
+                in_=planes[(a, j)][:].indirect(offsets[:, n0 // 16 : n1 // 16]),
+            )
+
+        def quantize_x(a, n0, n1):
+            nc.vector.quantize_mx(
+                out=x_codes[a][:, n0:n1].bitcast(FP8X4),
+                scales=x_scales[a][:, n0:n1],
+                in_=x_grouped[a][:, n0:n1, :].rearrange("p n j -> p (n j)"),
+            )
+
+        w_grouped = {}
+        w_codes = {}
+        w_scales = {}
+
+        def interleave_w(a, c, width, engine):
+            wg = keep.tile([P, width, PACK], BF16, align_bytes=64, name=f"wg_{a}_{c}")
+            dst = wg[:].rearrange("p (c i) j -> p c j i", i=4)
+            src = raws[(a, c)][:].rearrange("p j (c i) -> p c j i", i=4)
+            if engine == "s":
+                nc.scalar.copy(dst, src)
+            else:
+                nc.vector.tensor_copy(dst, src)
+            w_grouped[(a, c)] = wg
+
+        def quantize_w(a, c, width):
+            wc = keep.tile([P, width], U32, align_bytes=64, name=f"wc_{a}_{c}")
+            ws = keep.tile([P, width], U8, align_bytes=64, name=f"ws_{a}_{c}")
+            nc.vector.quantize_mx(
+                out=wc[:].bitcast(FP8X4), scales=ws[:], in_=w_grouped[(a, c)][:].rearrange("p n j -> p (n j)")
+            )
+            for m in range(c // P, (c + width) // P):
+                cols = slice(m * P - c, (m + 1) * P - c)
+                w_codes[(a, m)] = wc[:, cols].bitcast(FP8X4)
+                w_scales[(a, m)] = ws[:, cols]
+
+        acc = {}
+        for m in range(M_TILES):
+            for n0, n1 in [(0, S)] if m < M_TILES - 1 else [(0, HALF), (HALF, S)]:
+                bank = psum.tile([P, n1 - n0], F32, name=f"acc_{m}_{n0}")
+                acc[(m, n0)] = bank
+
+        pooled = keep.tile([P, M_TILES, V], F32, name="pooled")
+
+        def multiply(a, m):
+            for n0, n1 in [(0, S)] if m < M_TILES - 1 else [(0, HALF), (HALF, S)]:
+                nc.tensor.matmul_mx(
+                    out=acc[(m, n0)][:],
+                    lhsT=w_codes[(a, m)],
+                    lhsT_scale=w_scales[(a, m)],
+                    rhs=x_codes[a][:, n0:n1].bitcast(FP8X4),
+                    rhs_scale=x_scales[a][:, n0:n1],
+                    start=(a == 0),
+                    stop=(a == PASSES - 1),
+                )
+
+        def finish(m):
+            for n0, n1 in [(0, S)] if m < M_TILES - 1 else [(0, HALF), (HALF, S)]:
+                y = keep.tile([P, n1 - n0], F32, name=f"y_{m}_{n0}")
+                nc.scalar.activation(y[:], acc[(m, n0)][:], SILU, bias=bias[:, m : m + 1])
+                nc.vector.tensor_reduce(
+                    out=pooled[:, m, n0 // D : n1 // D], in_=y[:].rearrange("p (v d) -> p v d", d=D), axis=AX, op=MAX
+                )
+
+        out_view = out.rearrange("(t p) v -> p t v", p=P)
+
+        gather(0, 0, 0, S)
+        gather(0, 1, 0, S)
+        interleave_w(0, 0, 256, "s")
+        quantize_w(0, 0, 256)
+        gather(0, 2, 0, S)
+        gather(0, 3, 0, S)
+        quantize_x(0, 0, S)
+        multiply(0, 0)
+        multiply(0, 1)
+        gather(1, 0, 0, S)
+        gather(1, 1, 0, S)
+        gather(1, 2, 0, S)
+        gather(1, 3, 0, HALF)
+        gather(1, 3, HALF, S)
+        interleave_w(1, 0, 256, "s")
+        quantize_x(1, 0, HALF)
+        quantize_x(1, HALF, S)
+        quantize_w(1, 0, 256)
+        multiply(1, 0)
+        multiply(1, 1)
+        interleave_w(0, 256, 256, "v")
+        finish(0)
+        finish(1)
+        quantize_w(0, 256, 256)
+        multiply(0, 2)
+        multiply(0, 3)
+        interleave_w(1, 256, 128, "v")
+        quantize_w(1, 256, 128)
+        multiply(1, 2)
+        finish(2)
+        interleave_w(1, 384, 128, "v")
+        quantize_w(1, 384, 128)
+        multiply(1, 3)
+        nc.sync.dma_start(out=out_view[:, 0 : M_TILES - 1, :], in_=pooled[:, 0 : M_TILES - 1, :])
+        finish(3)
+        nc.sync.dma_start(out=out_view[:, M_TILES - 1, :], in_=pooled[:, M_TILES - 1, :])

@@ -22,13 +22,18 @@ K_PASS = P * PACK
 PASSES = K // K_PASS
 M_TILES = N // P
 HALF = S // 2
+HALVED = (0, 3)
 
 LOADS = (
-    [("x", 0, 0), ("x", 0, 1)]
-    + [("w", 0, 0, 256)]
-    + [("x", 0, 2), ("x", 0, 3), ("x", 1, 0), ("x", 1, 1), ("x", 1, 2), ("x", 1, 3)]
-    + [("w", 1, 0, 256), ("w", 0, 256, 256), ("w", 1, 256, 128), ("w", 1, 384, 128)]
+    [("x", 0, 0, 1, 0), ("x", 0, 1, 2, 1), ("x", 0, 2, 3, 0), ("x", 0, 3, 4, 1)]
+    + [("x", 1, 0, 1, 0), ("x", 1, 1, 2, 1), ("x", 1, 2, 3, 0)]
+    + [("w", 0, 0, 512, 1)]
+    + [("x", 1, 3, 4, 0), ("w", 1, 0, 256, 0), ("w", 1, 256, 128, 0), ("w", 1, 384, 128, 0)]
 )
+
+
+def token_parts(m):
+    return [(0, HALF), (HALF, S)] if m in HALVED else [(0, S)]
 
 
 def tile_picked_pool_lin_silu_sub_e_kernel(tc, xT, w, b, offs, out):
@@ -40,20 +45,26 @@ def tile_picked_pool_lin_silu_sub_e_kernel(tc, xT, w, b, offs, out):
         offsets = keep.tile([P, S // 16], U16, name="offsets")
         nc.sync.dma_start(offsets[:], offs)
 
+        b_rows = keep.tile([P, P], F32, name="b_rows")
+        nc.gpsimd.memset(b_rows[:], 0.0)
+        nc.gpsimd.dma_start(out=b_rows[0:M_TILES, :], in_=b.rearrange("(t p) o -> t (p o)", t=M_TILES))
+
+        queues = (nc.sync, nc.scalar)
         planes = {}
         raws = {}
         for item in LOADS:
             a = item[1]
             rows = slice(a * K_PASS, (a + 1) * K_PASS)
             if item[0] == "x":
-                j = item[2]
-                plane = keep.tile([P, T], F32, name=f"plane_{a}_{j}")
-                nc.sync.dma_start(out=plane[:], in_=xT[rows, :].rearrange("(p j) t -> p j t", j=PACK)[:, j, :])
-                planes[(a, j)] = plane
+                j0, j1 = item[2], item[3]
+                table = keep.tile([P, j1 - j0, T], F32, name=f"table_{a}_{j0}")
+                queues[item[4]].dma_start(out=table[:], in_=xT[rows, :].rearrange("(p j) t -> p j t", j=PACK)[:, j0:j1, :])
+                for j in range(j0, j1):
+                    planes[(a, j)] = table[:, j - j0, :]
             else:
                 c, width = item[2], item[3]
                 raw = keep.tile([P, PACK, width], F32, name=f"raw_{a}_{c}")
-                nc.sync.dma_start(out=raw[:], in_=w[rows, c : c + width].rearrange("(p j) n -> p j n", j=PACK))
+                queues[item[4]].dma_start(out=raw[:], in_=w[rows, c : c + width].rearrange("(p j) n -> p j n", j=PACK))
                 raws[(a, c)] = raw
 
         warm = keep.tile([P, 1], F32, name="warm")
@@ -62,11 +73,8 @@ def tile_picked_pool_lin_silu_sub_e_kernel(tc, xT, w, b, offs, out):
         nc.scalar.activation(warm_out[:], warm[:], SILU)
 
         ident = keep.tile([P, P], F32, name="ident")
-        b_rows = keep.tile([P, P], F32, name="b_rows")
         bias = keep.tile([P, M_TILES], F32, name="bias")
-        nc.gpsimd.memset(b_rows[:], 0.0)
         make_identity(nc, ident[:])
-        nc.scalar.dma_start(out=b_rows[0:M_TILES, :], in_=b.rearrange("(t p) o -> t (p o)", t=M_TILES))
         b_cols = psum.tile([P, P], F32, name="b_cols")
         nc.tensor.transpose(b_cols[:], b_rows[:], ident[:])
         nc.vector.tensor_copy(bias[:], b_cols[:, 0:M_TILES])
@@ -85,7 +93,7 @@ def tile_picked_pool_lin_silu_sub_e_kernel(tc, xT, w, b, offs, out):
         def gather(a, j, n0, n1):
             nc.vector.tensor_copy(
                 out=x_grouped[a][:, n0:n1, j],
-                in_=planes[(a, j)][:].indirect(offsets[:, n0 // 16 : n1 // 16]),
+                in_=planes[(a, j)].indirect(offsets[:, n0 // 16 : n1 // 16]),
             )
 
         def quantize_x(a, n0, n1):
@@ -95,94 +103,97 @@ def tile_picked_pool_lin_silu_sub_e_kernel(tc, xT, w, b, offs, out):
                 in_=x_grouped[a][:, n0:n1, :].rearrange("p n j -> p (n j)"),
             )
 
-        w_grouped = {}
-        w_codes = {}
-        w_scales = {}
+        w_grouped = []
+        w_codes = []
+        w_scales = []
+        for a in range(PASSES):
+            wg = keep.tile([P, N, PACK], BF16, align_bytes=64, name=f"wg_{a}")
+            wc = keep.tile([P, N], U32, align_bytes=64, name=f"wc_{a}")
+            ws = keep.tile([P, N], U8, align_bytes=64, name=f"ws_{a}")
+            w_grouped.append(wg)
+            w_codes.append(wc)
+            w_scales.append(ws)
 
-        def interleave_w(a, c, width, engine):
-            wg = keep.tile([P, width, PACK], BF16, align_bytes=64, name=f"wg_{a}_{c}")
-            dst = wg[:].rearrange("p (c i) j -> p c j i", i=4)
-            src = raws[(a, c)][:].rearrange("p j (c i) -> p c j i", i=4)
-            if engine == "s":
-                nc.scalar.copy(dst, src)
-            else:
-                nc.vector.tensor_copy(dst, src)
-            w_grouped[(a, c)] = wg
+        def interleave_w(copy, a, c0, c1):
+            for (pass_, first), raw in raws.items():
+                if pass_ == a and first <= c0 and c1 <= first + raw.shape[2]:
+                    copy(
+                        w_grouped[a][:, c0:c1, :].rearrange("p (c i) j -> p c j i", i=4),
+                        raw[:, :, c0 - first : c1 - first].rearrange("p j (c i) -> p c j i", i=4),
+                    )
 
-        def quantize_w(a, c, width):
-            wc = keep.tile([P, width], U32, align_bytes=64, name=f"wc_{a}_{c}")
-            ws = keep.tile([P, width], U8, align_bytes=64, name=f"ws_{a}_{c}")
+        def quantize_w(a, c0, c1):
             nc.vector.quantize_mx(
-                out=wc[:].bitcast(FP8X4), scales=ws[:], in_=w_grouped[(a, c)][:].rearrange("p n j -> p (n j)")
+                out=w_codes[a][:, c0:c1].bitcast(FP8X4),
+                scales=w_scales[a][:, c0:c1],
+                in_=w_grouped[a][:, c0:c1, :].rearrange("p n j -> p (n j)"),
             )
-            for m in range(c // P, (c + width) // P):
-                cols = slice(m * P - c, (m + 1) * P - c)
-                w_codes[(a, m)] = wc[:, cols].bitcast(FP8X4)
-                w_scales[(a, m)] = ws[:, cols]
 
         acc = {}
         for m in range(M_TILES):
-            for n0, n1 in [(0, S)] if m < M_TILES - 1 else [(0, HALF), (HALF, S)]:
+            for n0, n1 in token_parts(m):
                 bank = psum.tile([P, n1 - n0], F32, name=f"acc_{m}_{n0}")
                 acc[(m, n0)] = bank
 
         pooled = keep.tile([P, M_TILES, V], F32, name="pooled")
 
-        def multiply(a, m):
-            for n0, n1 in [(0, S)] if m < M_TILES - 1 else [(0, HALF), (HALF, S)]:
+        def multiply(a, m, parts=None):
+            for n0, n1 in parts or token_parts(m):
                 nc.tensor.matmul_mx(
                     out=acc[(m, n0)][:],
-                    lhsT=w_codes[(a, m)],
-                    lhsT_scale=w_scales[(a, m)],
+                    lhsT=w_codes[a][:, m * P : (m + 1) * P].bitcast(FP8X4),
+                    lhsT_scale=w_scales[a][:, m * P : (m + 1) * P],
                     rhs=x_codes[a][:, n0:n1].bitcast(FP8X4),
                     rhs_scale=x_scales[a][:, n0:n1],
                     start=(a == 0),
                     stop=(a == PASSES - 1),
                 )
 
-        def finish(m):
-            for n0, n1 in [(0, S)] if m < M_TILES - 1 else [(0, HALF), (HALF, S)]:
+        def finish(m, parts=None):
+            for n0, n1 in parts or token_parts(m):
                 y = keep.tile([P, n1 - n0], F32, name=f"y_{m}_{n0}")
                 nc.scalar.activation(y[:], acc[(m, n0)][:], SILU, bias=bias[:, m : m + 1])
                 nc.vector.tensor_reduce(
                     out=pooled[:, m, n0 // D : n1 // D], in_=y[:].rearrange("p (v d) -> p v d", d=D), axis=AX, op=MAX
                 )
 
+        s_copy = nc.scalar.copy
+        v_copy = nc.vector.tensor_copy
         out_view = out.rearrange("(t p) v -> p t v", p=P)
 
         gather(0, 0, 0, S)
         gather(0, 1, 0, S)
-        interleave_w(0, 0, 256, "s")
-        quantize_w(0, 0, 256)
         gather(0, 2, 0, S)
         gather(0, 3, 0, S)
+        interleave_w(s_copy, 0, 0, N)
         quantize_x(0, 0, S)
-        multiply(0, 0)
-        multiply(0, 1)
         gather(1, 0, 0, S)
+        quantize_w(0, 0, N)
+        for m in range(M_TILES):
+            multiply(0, m)
         gather(1, 1, 0, S)
         gather(1, 2, 0, S)
         gather(1, 3, 0, HALF)
         gather(1, 3, HALF, S)
-        interleave_w(1, 0, 256, "s")
+        interleave_w(s_copy, 1, 0, 128)
+        interleave_w(s_copy, 1, 128, 256)
         quantize_x(1, 0, HALF)
+        quantize_w(1, 0, 128)
+        multiply(1, 0, [(0, HALF)])
+        finish(0, [(0, HALF)])
         quantize_x(1, HALF, S)
-        quantize_w(1, 0, 256)
-        multiply(1, 0)
+        multiply(1, 0, [(HALF, S)])
+        finish(0, [(HALF, S)])
+        quantize_w(1, 128, 256)
         multiply(1, 1)
-        interleave_w(0, 256, 256, "v")
-        finish(0)
-        finish(1)
-        quantize_w(0, 256, 256)
-        multiply(0, 2)
-        multiply(0, 3)
-        interleave_w(1, 256, 128, "v")
-        quantize_w(1, 256, 128)
+        interleave_w(v_copy, 1, 256, 384)
+        quantize_w(1, 256, 384)
         multiply(1, 2)
-        finish(2)
-        interleave_w(1, 384, 128, "v")
-        quantize_w(1, 384, 128)
+        finish(1)
+        interleave_w(v_copy, 1, 384, 512)
+        quantize_w(1, 384, 512)
         multiply(1, 3)
+        finish(2)
         nc.sync.dma_start(out=out_view[:, 0 : M_TILES - 1, :], in_=pooled[:, 0 : M_TILES - 1, :])
         finish(3)
         nc.sync.dma_start(out=out_view[:, M_TILES - 1, :], in_=pooled[:, M_TILES - 1, :])

from contextlib import ExitStack

import concourse.mybir as mybir
from concourse.masks import make_identity

K, T, D, S, V, N = 1024, 2048, 16, 512, 32, 512
FLOPS = 2 * K * N * S

F32 = mybir.dt.float32
BF16 = mybir.dt.bfloat16
U32 = mybir.dt.uint32
U16 = mybir.dt.uint16
U8 = mybir.dt.uint8
FP8X4 = mybir.dt.float8_e4m3fn_x4
SILU = mybir.ActivationFunctionType.Silu
AX = mybir.AxisListType.X
MAX = mybir.AluOpType.max

P = 128
PACK = 4
K_PASS = P * PACK
PASSES = K // K_PASS
M_TILES = N // P
HALF = S // 2
HALVED = (0, 3)

LOADS = (
    [("x", 0, 0, 1, 0), ("x", 0, 1, 2, 1), ("x", 0, 2, 3, 0), ("x", 0, 3, 4, 1)]
    + [("x", 1, 0, 1, 0), ("x", 1, 1, 2, 1), ("x", 1, 2, 3, 0)]
    + [("w", 0, 0, 512, 1)]
    + [("x", 1, 3, 4, 0), ("w", 1, 0, 256, 0), ("w", 1, 256, 128, 0), ("w", 1, 384, 128, 0)]
)


def token_parts(m):
    return [(0, HALF), (HALF, S)] if m in HALVED else [(0, S)]


def tile_picked_pool_lin_silu_sub_e_kernel(tc, xT, w, b, offs, out):
    nc = tc.nc
    with ExitStack() as ctx:
        keep = ctx.enter_context(tc.tile_pool(name="keep", bufs=1))
        psum = ctx.enter_context(tc.psum_pool(name="psum", bufs=1))

        offsets = keep.tile([P, S // 16], U16, name="offsets")
        nc.sync.dma_start(offsets[:], offs)

        b_rows = keep.tile([P, P], F32, name="b_rows")
        nc.gpsimd.memset(b_rows[:], 0.0)
        nc.gpsimd.dma_start(out=b_rows[0:M_TILES, :], in_=b.rearrange("(t p) o -> t (p o)", t=M_TILES))

        queues = (nc.sync, nc.scalar)
        planes = {}
        raws = {}
        for item in LOADS:
            a = item[1]
            rows = slice(a * K_PASS, (a + 1) * K_PASS)
            if item[0] == "x":
                j0, j1 = item[2], item[3]
                table = keep.tile([P, j1 - j0, T], F32, name=f"table_{a}_{j0}")
                queues[item[4]].dma_start(out=table[:], in_=xT[rows, :].rearrange("(p j) t -> p j t", j=PACK)[:, j0:j1, :])
                for j in range(j0, j1):
                    planes[(a, j)] = table[:, j - j0, :]
            else:
                c, width = item[2], item[3]
                raw = keep.tile([P, PACK, width], F32, name=f"raw_{a}_{c}")
                queues[item[4]].dma_start(out=raw[:], in_=w[rows, c : c + width].rearrange("(p j) n -> p j n", j=PACK))
                raws[(a, c)] = raw

        warm = keep.tile([P, 1], F32, name="warm")
        warm_out = keep.tile([P, 1], F32, name="warm_out")
        nc.vector.memset(warm[:], 0.0)
        nc.scalar.activation(warm_out[:], warm[:], SILU)

        ident = keep.tile([P, P], F32, name="ident")
        bias = keep.tile([P, M_TILES], F32, name="bias")
        make_identity(nc, ident[:])
        b_cols = psum.tile([P, P], F32, name="b_cols")
        nc.tensor.transpose(b_cols[:], b_rows[:], ident[:])
        nc.vector.tensor_copy(bias[:], b_cols[:, 0:M_TILES])

        x_grouped = []
        x_codes = []
        x_scales = []
        for a in range(PASSES):
            xg = keep.tile([P, S, PACK], BF16, align_bytes=64, name=f"xg_{a}")
            xc = keep.tile([P, S], U32, align_bytes=64, name=f"xc_{a}")
            xs = keep.tile([P, S], U8, align_bytes=64, name=f"xs_{a}")
            x_grouped.append(xg)
            x_codes.append(xc)
            x_scales.append(xs)

        def gather(a, j, n0, n1):
            nc.vector.tensor_copy(
                out=x_grouped[a][:, n0:n1, j],
                in_=planes[(a, j)].indirect(offsets[:, n0 // 16 : n1 // 16]),
            )

        def quantize_x(a, n0, n1):
            nc.vector.quantize_mx(
                out=x_codes[a][:, n0:n1].bitcast(FP8X4),
                scales=x_scales[a][:, n0:n1],
                in_=x_grouped[a][:, n0:n1, :].rearrange("p n j -> p (n j)"),
            )

        w_grouped = []
        w_codes = []
        w_scales = []
        for a in range(PASSES):
            wg = keep.tile([P, N, PACK], BF16, align_bytes=64, name=f"wg_{a}")
            wc = keep.tile([P, N], U32, align_bytes=64, name=f"wc_{a}")
            ws = keep.tile([P, N], U8, align_bytes=64, name=f"ws_{a}")
            w_grouped.append(wg)
            w_codes.append(wc)
            w_scales.append(ws)

        def interleave_w(copy, a, c0, c1):
            for (pass_, first), raw in raws.items():
                if pass_ == a and first <= c0 and c1 <= first + raw.shape[2]:
                    copy(
                        w_grouped[a][:, c0:c1, :].rearrange("p (c i) j -> p c j i", i=4),
                        raw[:, :, c0 - first : c1 - first].rearrange("p j (c i) -> p c j i", i=4),
                    )

        def quantize_w(a, c0, c1):
            nc.vector.quantize_mx(
                out=w_codes[a][:, c0:c1].bitcast(FP8X4),
                scales=w_scales[a][:, c0:c1],
                in_=w_grouped[a][:, c0:c1, :].rearrange("p n j -> p (n j)"),
            )

        acc = {}
        for m in range(M_TILES):
            for n0, n1 in token_parts(m):
                bank = psum.tile([P, n1 - n0], F32, name=f"acc_{m}_{n0}")
                acc[(m, n0)] = bank

        pooled = keep.tile([P, M_TILES, V], F32, name="pooled")

        def multiply(a, m, parts=None):
            for n0, n1 in parts or token_parts(m):
                nc.tensor.matmul_mx(
                    out=acc[(m, n0)][:],
                    lhsT=w_codes[a][:, m * P : (m + 1) * P].bitcast(FP8X4),
                    lhsT_scale=w_scales[a][:, m * P : (m + 1) * P],
                    rhs=x_codes[a][:, n0:n1].bitcast(FP8X4),
                    rhs_scale=x_scales[a][:, n0:n1],
                    start=(a == 0),
                    stop=(a == PASSES - 1),
                )

        def finish(m, parts=None):
            for n0, n1 in parts or token_parts(m):
                y = keep.tile([P, n1 - n0], F32, name=f"y_{m}_{n0}")
                nc.scalar.activation(y[:], acc[(m, n0)][:], SILU, bias=bias[:, m : m + 1])
                nc.vector.tensor_reduce(
                    out=pooled[:, m, n0 // D : n1 // D], in_=y[:].rearrange("p (v d) -> p v d", d=D), axis=AX, op=MAX
                )

        s_copy = nc.scalar.copy
        v_copy = nc.vector.tensor_copy
        out_view = out.rearrange("(t p) v -> p t v", p=P)

        gather(0, 0, 0, S)
        gather(0, 1, 0, S)
        gather(0, 2, 0, S)
        gather(0, 3, 0, S)
        interleave_w(s_copy, 0, 0, N)
        quantize_x(0, 0, S)
        gather(1, 0, 0, S)
        quantize_w(0, 0, N)
        for m in range(M_TILES):
            multiply(0, m)
        gather(1, 1, 0, S)
        gather(1, 2, 0, S)
        gather(1, 3, 0, HALF)
        gather(1, 3, HALF, S)
        interleave_w(s_copy, 1, 0, 128)
        interleave_w(s_copy, 1, 128, 256)
        quantize_x(1, 0, HALF)
        quantize_w(1, 0, 128)
        multiply(1, 0, [(0, HALF)])
        finish(0, [(0, HALF)])
        quantize_x(1, HALF, S)
        multiply(1, 0, [(HALF, S)])
        finish(0, [(HALF, S)])
        quantize_w(1, 128, 256)
        multiply(1, 1)
        interleave_w(v_copy, 1, 256, 384)
        quantize_w(1, 256, 384)
        multiply(1, 2)
        finish(1)
        interleave_w(v_copy, 1, 384, 512)
        quantize_w(1, 384, 512)
        multiply(1, 3)
        finish(2)
        nc.sync.dma_start(out=out_view[:, 0 : M_TILES - 1, :], in_=pooled[:, 0 : M_TILES - 1, :])
        finish(3)
        nc.sync.dma_start(out=out_view[:, M_TILES - 1, :], in_=pooled[:, M_TILES - 1, :])
